import numpy as np
import ml_dtypes


def mxq(x, axis, fmt="e4m3"):
    dtype, down = {"e4m3": (ml_dtypes.float8_e4m3fn, 7), "e5m2": (ml_dtypes.float8_e5m2, 14)}[fmt]
    v = np.moveaxis(np.asarray(x, np.float32).astype(ml_dtypes.bfloat16).astype(np.float64), axis, -1)
    blocks = v.reshape(v.shape[:-1] + (-1, 32))
    amax = np.abs(blocks).max(-1, keepdims=True)
    byte = np.maximum(np.where(amax > 0, np.frexp(amax)[1] - 1 + 127, 0) - down, 1)
    scale = np.exp2(byte - 127.0)
    codes = (blocks / scale).astype(np.float32).astype(dtype).astype(np.float64)
    return np.moveaxis((codes * scale).reshape(v.shape), -1, axis)


WIDE = False


def mx_kscale(k):
    if not WIDE:
        return np.ones(k)
    levels = np.array([10, -10, 5, -5, 0])
    if k % 512:
        return np.exp2(np.random.permutation(np.resize(levels, k // 32))).repeat(32)
    a = np.empty((k // 512, 16))
    for p in range(k // 512):
        a[p, :8] = np.random.permutation(np.resize(levels, 8))
        for g in range(8):
            far = levels[np.abs(levels - a[p, g]) >= 10]
            a[p, g + 8] = far[np.random.randint(len(far))]
    return np.exp2(a.ravel()).repeat(32)


BF16 = ml_dtypes.bfloat16


def bf(x):
    return np.asarray(x, np.float32).astype(BF16)


def f64(x):
    return np.asarray(x).astype(np.float64)


E2M1 = np.array([0.0, 0.5, 1.0, 1.5, 2.0, 3.0, 4.0, 6.0, -0.0, -0.5, -1.0, -1.5, -2.0, -3.0, -4.0, -6.0])


def pack_weight(w, fmt):
    k, n = w.shape
    w = f64(bf(w)).reshape(k // 32, 32, n)
    amax = np.abs(w).max(1)
    if fmt == "e4m3":
        byte = np.frexp(amax)[1] - 1 + 127 - 7
    else:
        mant, ex = np.frexp(amax / 6.0)
        byte = np.where(mant > 0.5, ex, ex - 1) + 127
    byte = np.clip(np.where(amax > 0, byte, 1), 1, 254)
    scaled = (w * np.exp2(127.0 - byte)[:, None, :]).reshape(k, n).astype(np.float32)
    by_word = np.ascontiguousarray(scaled.reshape(k // 512, 128, 4, n).transpose(0, 1, 3, 2))
    if fmt == "e4m3":
        words = by_word.astype(ml_dtypes.float8_e4m3fn).view(np.uint8)
    else:
        c = by_word.astype(ml_dtypes.float4_e2m1fn).view(np.uint8) & 0xF
        words = c[..., 0::2] | (c[..., 1::2] << 4)
    return np.ascontiguousarray(words), np.ascontiguousarray(byte.astype(np.uint8).reshape(k // 512, 16, n))


def unpack_weight(words, scales, fmt):
    g, p, n, _ = words.shape
    if fmt == "e4m3":
        vals = np.ascontiguousarray(words).view(ml_dtypes.float8_e4m3fn).astype(np.float64)
    else:
        nib = np.empty((g, p, n, 4), np.uint8)
        nib[..., 0::2] = words & 0xF
        nib[..., 1::2] = words >> 4
        vals = E2M1[nib]
    vals = vals * np.repeat(np.exp2(scales.astype(np.float64) - 127.0), 8, axis=1)[..., None]
    return vals.transpose(0, 1, 3, 2).reshape(g * 512, n)
def pack4(w):
    words, scales = pack_weight(w, "e2m1")
    return words.reshape(words.shape[0], 128, -1), scales


def unpack4(words, scales):
    return unpack_weight(words.reshape(words.shape[0], 128, -1, 2), scales, "e2m1")


K, T, P = 512, 2048, 2048


def setup_inputs():
    s = mx_kscale(K)
    u = mx_kscale(T)
    a = np.random.standard_normal((K, P))
    c = np.random.standard_normal((K, T))
    a_words, a_scales = pack4(a * s[:, None])
    c_words, c_scales = pack4(c / np.sqrt(K) / s[:, None])
    d_words, d_scales = pack_weight(c.T / np.sqrt(T) / u[:, None], "e4m3")
    return {"movie": bf(np.random.standard_normal((T, P))),
            "a_words": a_words, "a_scales": a_scales,
            "c_words": c_words, "c_scales": c_scales,
            "frame_weight": bf((1 + 0.1 * np.random.standard_normal(T)) * u),
            "d_words": d_words, "d_scales": d_scales,
            "step": bf(1 + 0.1 * np.random.standard_normal(K))}


def reference(movie, a_words, a_scales, c_words, c_scales, frame_weight, d_words, d_scales, step):
    a = unpack4(a_words, a_scales)
    c = unpack4(c_words, c_scales)
    d = unpack_weight(d_words, d_scales, "e4m3")
    model = c.T @ a
    h = (f64(movie) - model) * f64(frame_weight)[:, None]
    g = d.T @ mxq(h, 0, "e4m3")
    return g * f64(step)[:, None]

@@ -1,0 +1,253 @@
+from contextlib import ExitStack
+
+import concourse.mybir as mybir
+
+K, T, PIX = 512, 2048, 2048
+FLOPS = 2 * 2 * K * T * PIX
+
+F32 = mybir.dt.float32
+BF16 = mybir.dt.bfloat16
+I32 = mybir.dt.int32
+U32 = mybir.dt.uint32
+U8 = mybir.dt.uint8
+FP8X4 = mybir.dt.float8_e4m3fn_x4
+FP4X4 = mybir.dt.float4_e2m1fn_x4
+ALU = mybir.AluOpType
+COPY = mybir.ActivationFunctionType.Copy
+
+P = 128
+PACK = 4
+N = 512
+GROUPS = T // (P * PACK)
+CHUNKS = PIX // N
+M_TILES = K // P
+STEPS = GROUPS * CHUNKS
+POOL_PIX = 384
+LAST_VEC_PIX = 256
+MW_BUFS = 12
+HS_BUFS = 3
+OUT_BUFS = 8
+VEC_MW_STEPS = (7, 8, 10, 11, 13, 14, 15)
+
+
+def tile_calcium_residual_demixing_s4_kernel(
+    tc, movie, a_words, a_scales, c_words, c_scales, frame_weight, d_words, d_scales, step, out
+):
+    nc = tc.nc
+    with ExitStack() as ctx:
+        sb = ctx.enter_context(tc.tile_pool(name="sb", bufs=1))
+        ps = ctx.enter_context(tc.psum_pool(name="ps", bufs=1))
+        ctx.enter_context(tc.manual_schedule())
+
+        def sbuf(name, shape, dtype):
+            return sb.tile(shape, dtype, name=name, align_bytes=64)
+
+        c_raw0 = sbuf("c_raw0", [P, 2 * N], U8)
+        c_raw1 = sbuf("c_raw1", [P, (GROUPS - 1) * 2 * N], U8)
+        cs_raw = sbuf("cs_raw", [P, T], U8)
+        c_codes = [sbuf("c_codes%d" % g, [P, 2 * N], U8) for g in range(GROUPS)]
+        c_plane = [sbuf("c_plane%d" % g, [P, N], U8) for g in range(GROUPS)]
+        a_codes0 = sbuf("a_codes0", [P, 2 * N], U8)
+        a_codes1 = sbuf("a_codes1", [P, (CHUNKS - 1) * 2 * N], U8)
+        a_plane = sbuf("a_plane", [P, PIX], U8)
+        d_codes = sbuf("d_codes", [P, GROUPS, K], U32)
+        d_plane = sbuf("d_plane", [P, GROUPS, K], U8)
+        fw_raw = sbuf("fw_raw", [P, GROUPS, 16], BF16)
+        neg_fw = sbuf("neg_fw", [P, GROUPS, PACK], F32)
+        step_raw = sbuf("step_raw", [P, M_TILES, 16], BF16)
+        step_f32 = sbuf("step_f32", [P, M_TILES], F32)
+        warm_in = sbuf("warm_in", [P, 1], F32)
+        warm_out = sbuf("warm_out", [P, 1], F32)
+        mv = [sbuf("mv%d" % s, [P, PACK, N], BF16) for s in range(STEPS)]
+        mw = [sbuf("mw%d" % i, [P, N], F32) for i in range(MW_BUFS)]
+        hs = [sbuf("hs%d" % i, [P, PACK, N], BF16) for i in range(HS_BUFS)]
+        g_pool = sbuf("g_pool", [P, POOL_PIX, PACK], BF16)
+        g_act = [sbuf("g_act%d" % i, [P, N - LAST_VEC_PIX, PACK], BF16) for i in range(2)]
+        h_codes = [sbuf("h_codes%d" % s, [P, N], U32) for s in range(STEPS)]
+        h_plane = [sbuf("h_plane%d" % s, [P, N], U8) for s in range(STEPS)]
+        res = [sbuf("res%d" % i, [P, N], F32) for i in range(OUT_BUFS)]
+        e_bank = [ps.tile([P, N], F32, name="e_bank%d" % t) for t in range(PACK)]
+        o_bank = [ps.tile([P, N], F32, name="o_bank%d" % m) for m in range(M_TILES)]
+
+        def load_movie(s):
+            c, g = divmod(s, GROUPS)
+            rows = movie[g * N : (g + 1) * N, c * N : (c + 1) * N]
+            nc.sync.dma_start(out=mv[s][:], in_=rows.rearrange("(p t) n -> p t n", t=PACK))
+
+        def load_plane(plane, rows):
+            for r in range(4):
+                nc.sync.dma_start(out=plane[r:P:32].bitcast(I32), in_=rows[r:16:4].bitcast(I32))
+
+        def order_c_codes(g):
+            raw = c_raw0[:] if g == 0 else c_raw1[:, (g - 1) * 2 * N : g * 2 * N]
+            nc.vector.tensor_copy(
+                out=c_codes[g][:].rearrange("p (t m b) -> p t m b", t=PACK, b=2),
+                in_=raw.rearrange("p (m t b) -> p t m b", t=PACK, b=2),
+            )
+
+        def order_c_plane(g):
+            nc.vector.tensor_copy(
+                out=c_plane[g][:].rearrange("p (t m) -> p t m", t=PACK),
+                in_=cs_raw[:, g * N : (g + 1) * N].rearrange("p (m t) -> p t m", t=PACK),
+            )
+
+        def model(s, t):
+            c, g = divmod(s, GROUPS)
+            a_chunk = a_codes0[:] if c == 0 else a_codes1[:, (c - 1) * 2 * N : c * 2 * N]
+            nc.tensor.matmul_mx(
+                out=e_bank[t][:],
+                lhsT=c_codes[g][:, t * 2 * P : (t + 1) * 2 * P].bitcast(FP4X4),
+                lhsT_scale=c_plane[g][:, t * P : (t + 1) * P],
+                rhs=a_chunk.bitcast(FP4X4),
+                rhs_scale=a_plane[:, c * N : (c + 1) * N],
+                start=True,
+                stop=True,
+            )
+
+        def weigh_movie(s, t, on_vector):
+            g = s % GROUPS
+            dst = mw[(s * PACK + t) % MW_BUFS]
+            if on_vector:
+                nc.vector.tensor_scalar(
+                    out=dst[:], in0=mv[s][:, t, :], scalar1=neg_fw[:, g, t : t + 1], scalar2=None, op0=ALU.mult
+                )
+            else:
+                nc.scalar.activation(out=dst[:], in_=mv[s][:, t, :], func=COPY, scale=neg_fw[:, g, t : t + 1])
+
+        def weigh_on_scalar(s):
+            for t in range(PACK - 1 if s in VEC_MW_STEPS else PACK):
+                weigh_movie(s, t, False)
+
+        def residual(s, t):
+            g = s % GROUPS
+            nc.vector.scalar_tensor_tensor(
+                out=hs[s % HS_BUFS][:, t, :],
+                in0=e_bank[t][:],
+                scalar=neg_fw[:, g, t : t + 1],
+                in1=mw[(s * PACK + t) % MW_BUFS][:],
+                op0=ALU.mult,
+                op1=ALU.subtract,
+            )
+
+        def rows_of(s, lo, hi):
+            return hs[s % HS_BUFS][:, :, lo:hi].rearrange("p t n -> p n t")
+
+        def quantize(s, grouped, lo, hi, first):
+            nc.vector.quantize_mx(
+                out=h_codes[s][:, lo:hi].bitcast(FP8X4),
+                scales=h_plane[s][:, lo:hi],
+                in_=grouped[:, lo - first : hi - first, :].rearrange("p n t -> p (n t)"),
+            )
+
+        def quantize_step(s):
+            quantize(s, g_act[s % 2], POOL_PIX, N, POOL_PIX)
+            quantize(s, g_pool, 0, 256, 0)
+            quantize(s, g_pool, 256, POOL_PIX, 0)
+
+        def update(c, g, m):
+            s = c * GROUPS + g
+            nc.tensor.matmul_mx(
+                out=o_bank[m][:],
+                lhsT=d_codes[:, g, m * P : (m + 1) * P].bitcast(FP8X4),
+                lhsT_scale=d_plane[:, g, m * P : (m + 1) * P],
+                rhs=h_codes[s][:].bitcast(FP8X4),
+                rhs_scale=h_plane[s][:],
+                start=(g == 0),
+                stop=(g == GROUPS - 1),
+            )
+
+        def finish(c, m, on_vector):
+            dst = res[(c * M_TILES + m) % OUT_BUFS]
+            if on_vector:
+                nc.vector.tensor_scalar(
+                    out=dst[:], in0=o_bank[m][:], scalar1=step_f32[:, m : m + 1], scalar2=None, op0=ALU.mult
+                )
+            else:
+                nc.scalar.activation(out=dst[:], in_=o_bank[m][:], func=COPY, scale=step_f32[:, m : m + 1])
+            nc.sync.dma_start(out=out[m * P : (m + 1) * P, c * N : (c + 1) * N], in_=dst[:])
+
+        sums_at = {s: [] for s in range(STEPS)}
+        for m in range(M_TILES):
+            sums_at[5 + m].append((0, m))
+            sums_at[9 + m].append((1, m))
+            sums_at[13 + m // 2].append((2, m))
+
+        nc.vector.memset(cs_raw[:].bitcast(I32), 0)
+        nc.vector.memset(a_plane[:].bitcast(I32), 0)
+        nc.vector.memset(d_plane[:].rearrange("p g n -> p (g n)").bitcast(I32), 0)
+        nc.gpsimd.memset(warm_in[:], 0.0)
+        nc.scalar.activation(out=warm_out[:], in_=warm_in[:], func=COPY, scale=-1.0)
+
+        nc.sync.dma_start(out=c_raw0[:].bitcast(I32), in_=c_words[0][:, 0 : 2 * N].bitcast(I32))
+        nc.sync.dma_start(out=c_raw1[:].bitcast(I32), in_=c_words[0][:, 2 * N :].bitcast(I32))
+        load_plane(cs_raw, c_scales[0])
+        nc.sync.dma_start(out=fw_raw[:, :, 0:PACK], in_=frame_weight.rearrange("(g p t) -> p g t", g=GROUPS, t=PACK))
+        load_movie(0)
+        nc.sync.dma_start(out=a_codes0[:].bitcast(I32), in_=a_words[0][:, 0 : 2 * N].bitcast(I32))
+        load_plane(a_plane, a_scales[0])
+        load_movie(1)
+        load_movie(2)
+        nc.sync.dma_start(out=a_codes1[:].bitcast(I32), in_=a_words[0][:, 2 * N :].bitcast(I32))
+        load_movie(3)
+        load_plane(d_plane, d_scales.rearrange("g q n -> q g n"))
+        with nc.allow_non_contiguous_dma(reason="one step value for each partition"):
+            nc.sync.dma_start(out=step_raw[:, :, 0:1], in_=step.rearrange("(m p o) -> p m o", p=P, o=1))
+        load_movie(4)
+        nc.sync.dma_start(out=d_codes[:].bitcast(I32), in_=d_words.rearrange("g p n t -> p g (n t)").bitcast(I32))
+        for s in range(5, STEPS):
+            load_movie(s)
+
+        nc.scalar.activation(out=neg_fw[:], in_=fw_raw[:, :, 0:PACK], func=COPY, scale=-1.0)
+        order_c_codes(0)
+        order_c_codes(1)
+        order_c_plane(0)
+        for t in range(PACK):
+            model(0, t)
+        order_c_codes(2)
+        order_c_codes(3)
+        for g in range(1, GROUPS):
+            order_c_plane(g)
+        weigh_on_scalar(0)
+        weigh_on_scalar(1)
+
+        for s in range(STEPS):
+            passes = [(c, g, m) for (c, m) in sums_at[s] for g in range(GROUPS)]
+            if s == STEPS - 1:
+                passes = [(CHUNKS - 1, g, m) for g in range(2) for m in range(M_TILES)]
+            share = len(passes) // PACK
+            for item in passes[:share]:
+                update(*item)
+            for t in range(PACK):
+                residual(s, t)
+                for item in passes[(t + 1) * share : (t + 2) * share]:
+                    update(*item)
+                if s + 1 < STEPS:
+                    model(s + 1, t)
+            if s + 1 in VEC_MW_STEPS:
+                weigh_movie(s + 1, PACK - 1, True)
+            if s == STEPS - 1:
+                nc.scalar.copy(out=g_act[s % 2][:], in_=rows_of(s, LAST_VEC_PIX, N))
+            if s > 0:
+                quantize_step(s - 1)
+            if s < STEPS - 1:
+                nc.gpsimd.tensor_scalar(
+                    out=g_pool[:], in0=rows_of(s, 0, POOL_PIX), scalar1=1.0, scalar2=0.0, op0=ALU.mult, op1=ALU.add
+                )
+                nc.scalar.copy(out=g_act[s % 2][:, 0 : N - POOL_PIX, :], in_=rows_of(s, POOL_PIX, N))
+            if s == 3:
+                nc.scalar.activation(out=step_f32[:], in_=step_raw[:, :, 0], func=COPY)
+            for c, m in sums_at[s]:
+                finish(c, m, False)
+            if s + 2 < STEPS:
+                weigh_on_scalar(s + 2)
+
+        last = STEPS - 1
+        for m in range(M_TILES):
+            update(CHUNKS - 1, GROUPS - 2, m)
+        nc.vector.tensor_copy(out=g_pool[:, 0:LAST_VEC_PIX, :], in_=rows_of(last, 0, LAST_VEC_PIX))
+        quantize(last, g_act[last % 2], LAST_VEC_PIX, N, LAST_VEC_PIX)
+        quantize(last, g_pool, 0, LAST_VEC_PIX, 0)
+        for m in range(M_TILES):
+            update(CHUNKS - 1, GROUPS - 1, m)
+        for m in range(M_TILES):
+            finish(CHUNKS - 1, m, m % 2 == 0)

@@ -22,12 +22,14 @@ GROUPS = T // (P * PACK)
 CHUNKS = PIX // N
 M_TILES = K // P
 STEPS = GROUPS * CHUNKS
-POOL_PIX = 384
+POOL_PIX = 368
 LAST_VEC_PIX = 256
-MW_BUFS = 12
+MW_BUFS = 22
 HS_BUFS = 3
 OUT_BUFS = 8
-VEC_MW_STEPS = (7, 8, 10, 11, 13, 14, 15)
+VEC_MW = [(s, t) for s in range(1, 5) for t in (2, 3)]
+SCALAR_MW_HEAD = 13
+SCALAR_MW_AFTER = (4, 4, 4, 4, 4, 3, 3, 3, 3, 3, 3, 2, 2, 1, 0, 0)
 
 
 def tile_calcium_residual_demixing_s4_kernel(
@@ -61,8 +63,7 @@ def tile_calcium_residual_demixing_s4_kernel(
         mv = [sbuf("mv%d" % s, [P, PACK, N], BF16) for s in range(STEPS)]
         mw = [sbuf("mw%d" % i, [P, N], F32) for i in range(MW_BUFS)]
         hs = [sbuf("hs%d" % i, [P, PACK, N], BF16) for i in range(HS_BUFS)]
-        g_pool = sbuf("g_pool", [P, POOL_PIX, PACK], BF16)
-        g_act = [sbuf("g_act%d" % i, [P, N - LAST_VEC_PIX, PACK], BF16) for i in range(2)]
+        grouped = [sbuf("grouped%d" % i, [P, N, PACK], BF16) for i in range(2)]
         h_codes = [sbuf("h_codes%d" % s, [P, N], U32) for s in range(STEPS)]
         h_plane = [sbuf("h_plane%d" % s, [P, N], U8) for s in range(STEPS)]
         res = [sbuf("res%d" % i, [P, N], F32) for i in range(OUT_BUFS)]
@@ -114,8 +115,10 @@ def tile_calcium_residual_demixing_s4_kernel(
             else:
                 nc.scalar.activation(out=dst[:], in_=mv[s][:, t, :], func=COPY, scale=neg_fw[:, g, t : t + 1])
 
-        def weigh_on_scalar(s):
-            for t in range(PACK - 1 if s in VEC_MW_STEPS else PACK):
+        scalar_mw = [(s, t) for s in range(STEPS) for t in range(PACK) if (s, t) not in VEC_MW]
+
+        def weigh_on_scalar(first, count):
+            for s, t in scalar_mw[first : first + count]:
                 weigh_movie(s, t, False)
 
         def residual(s, t):
@@ -132,17 +135,18 @@ def tile_calcium_residual_demixing_s4_kernel(
         def rows_of(s, lo, hi):
             return hs[s % HS_BUFS][:, :, lo:hi].rearrange("p t n -> p n t")
 
-        def quantize(s, grouped, lo, hi, first):
+        def interleave_by_fours(engine_copy, s, lo, hi):
+            engine_copy(
+                out=grouped[s % 2][:, lo:hi, :].rearrange("p (c i) t -> p c t i", i=4),
+                in_=hs[s % HS_BUFS][:, :, lo:hi].rearrange("p t (c i) -> p c t i", i=4),
+            )
+
+        def quantize(s, lo, hi):
             nc.vector.quantize_mx(
                 out=h_codes[s][:, lo:hi].bitcast(FP8X4),
                 scales=h_plane[s][:, lo:hi],
-                in_=grouped[:, lo - first : hi - first, :].rearrange("p n t -> p (n t)"),
+                in_=grouped[s % 2][:, lo:hi, :].rearrange("p n t -> p (n t)"),
             )
-
-        def quantize_step(s):
-            quantize(s, g_act[s % 2], POOL_PIX, N, POOL_PIX)
-            quantize(s, g_pool, 0, 256, 0)
-            quantize(s, g_pool, 256, POOL_PIX, 0)
 
         def update(c, g, m):
             s = c * GROUPS + g
@@ -179,36 +183,33 @@ def tile_calcium_residual_demixing_s4_kernel(
         nc.scalar.activation(out=warm_out[:], in_=warm_in[:], func=COPY, scale=-1.0)
 
         nc.sync.dma_start(out=c_raw0[:].bitcast(I32), in_=c_words[0][:, 0 : 2 * N].bitcast(I32))
-        nc.sync.dma_start(out=c_raw1[:].bitcast(I32), in_=c_words[0][:, 2 * N :].bitcast(I32))
         load_plane(cs_raw, c_scales[0])
+        nc.sync.dma_start(out=c_raw1[:].bitcast(I32), in_=c_words[0][:, 2 * N :].bitcast(I32))
         nc.sync.dma_start(out=fw_raw[:, :, 0:PACK], in_=frame_weight.rearrange("(g p t) -> p g t", g=GROUPS, t=PACK))
         load_movie(0)
         nc.sync.dma_start(out=a_codes0[:].bitcast(I32), in_=a_words[0][:, 0 : 2 * N].bitcast(I32))
         load_plane(a_plane, a_scales[0])
-        load_movie(1)
-        load_movie(2)
+        for s in range(1, 6):
+            load_movie(s)
         nc.sync.dma_start(out=a_codes1[:].bitcast(I32), in_=a_words[0][:, 2 * N :].bitcast(I32))
-        load_movie(3)
+        load_movie(6)
         load_plane(d_plane, d_scales.rearrange("g q n -> q g n"))
         with nc.allow_non_contiguous_dma(reason="one step value for each partition"):
             nc.sync.dma_start(out=step_raw[:, :, 0:1], in_=step.rearrange("(m p o) -> p m o", p=P, o=1))
-        load_movie(4)
         nc.sync.dma_start(out=d_codes[:].bitcast(I32), in_=d_words.rearrange("g p n t -> p g (n t)").bitcast(I32))
-        for s in range(5, STEPS):
+        for s in range(7, STEPS):
             load_movie(s)
 
         nc.scalar.activation(out=neg_fw[:], in_=fw_raw[:, :, 0:PACK], func=COPY, scale=-1.0)
         order_c_codes(0)
-        order_c_codes(1)
         order_c_plane(0)
         for t in range(PACK):
             model(0, t)
-        order_c_codes(2)
-        order_c_codes(3)
+        for g in range(1, GROUPS):
+            order_c_codes(g)
         for g in range(1, GROUPS):
             order_c_plane(g)
-        weigh_on_scalar(0)
-        weigh_on_scalar(1)
+        weigh_on_scalar(0, SCALAR_MW_HEAD)
 
         for s in range(STEPS):
             passes = [(c, g, m) for (c, m) in sums_at[s] for g in range(GROUPS)]
@@ -219,34 +220,39 @@ def tile_calcium_residual_demixing_s4_kernel(
                 update(*item)
             for t in range(PACK):
                 residual(s, t)
+                if s == 0 and t in (1, 2):
+                    for item in VEC_MW[(t - 1) * 4 : t * 4]:
+                        weigh_movie(*item, True)
                 for item in passes[(t + 1) * share : (t + 2) * share]:
                     update(*item)
                 if s + 1 < STEPS:
                     model(s + 1, t)
-            if s + 1 in VEC_MW_STEPS:
-                weigh_movie(s + 1, PACK - 1, True)
-            if s == STEPS - 1:
-                nc.scalar.copy(out=g_act[s % 2][:], in_=rows_of(s, LAST_VEC_PIX, N))
             if s > 0:
-                quantize_step(s - 1)
+                quantize(s - 1, 0, N)
             if s < STEPS - 1:
                 nc.gpsimd.tensor_scalar(
-                    out=g_pool[:], in0=rows_of(s, 0, POOL_PIX), scalar1=1.0, scalar2=0.0, op0=ALU.mult, op1=ALU.add
+                    out=grouped[s % 2][:, 0:POOL_PIX, :],
+                    in0=rows_of(s, 0, POOL_PIX),
+                    scalar1=1.0,
+                    scalar2=0.0,
+                    op0=ALU.mult,
+                    op1=ALU.add,
                 )
-                nc.scalar.copy(out=g_act[s % 2][:, 0 : N - POOL_PIX, :], in_=rows_of(s, POOL_PIX, N))
+                interleave_by_fours(nc.scalar.copy, s, POOL_PIX, N)
+            else:
+                interleave_by_fours(nc.scalar.copy, s, LAST_VEC_PIX, N)
             if s == 3:
                 nc.scalar.activation(out=step_f32[:], in_=step_raw[:, :, 0], func=COPY)
             for c, m in sums_at[s]:
                 finish(c, m, False)
-            if s + 2 < STEPS:
-                weigh_on_scalar(s + 2)
+            weigh_on_scalar(SCALAR_MW_HEAD + sum(SCALAR_MW_AFTER[:s]), SCALAR_MW_AFTER[s])
 
         last = STEPS - 1
         for m in range(M_TILES):
             update(CHUNKS - 1, GROUPS - 2, m)
-        nc.vector.tensor_copy(out=g_pool[:, 0:LAST_VEC_PIX, :], in_=rows_of(last, 0, LAST_VEC_PIX))
-        quantize(last, g_act[last % 2], LAST_VEC_PIX, N, LAST_VEC_PIX)
-        quantize(last, g_pool, 0, LAST_VEC_PIX, 0)
+        interleave_by_fours(nc.vector.tensor_copy, last, 0, LAST_VEC_PIX)
+        quantize(last, LAST_VEC_PIX, N)
+        quantize(last, 0, LAST_VEC_PIX)
         for m in range(M_TILES):
             update(CHUNKS - 1, GROUPS - 1, m)
         for m in range(M_TILES):

from contextlib import ExitStack

import concourse.mybir as mybir

K, T, PIX = 512, 2048, 2048
FLOPS = 2 * 2 * K * T * PIX

F32 = mybir.dt.float32
BF16 = mybir.dt.bfloat16
I32 = mybir.dt.int32
U32 = mybir.dt.uint32
U8 = mybir.dt.uint8
FP8X4 = mybir.dt.float8_e4m3fn_x4
FP4X4 = mybir.dt.float4_e2m1fn_x4
ALU = mybir.AluOpType
COPY = mybir.ActivationFunctionType.Copy

P = 128
PACK = 4
N = 512
GROUPS = T // (P * PACK)
CHUNKS = PIX // N
M_TILES = K // P
STEPS = GROUPS * CHUNKS
POOL_PIX = 368
LAST_VEC_PIX = 256
MW_BUFS = 22
HS_BUFS = 3
OUT_BUFS = 8
VEC_MW = [(s, t) for s in range(1, 5) for t in (2, 3)]
SCALAR_MW_HEAD = 13
SCALAR_MW_AFTER = (4, 4, 4, 4, 4, 3, 3, 3, 3, 3, 3, 2, 2, 1, 0, 0)


def tile_calcium_residual_demixing_s4_kernel(
    tc, movie, a_words, a_scales, c_words, c_scales, frame_weight, d_words, d_scales, step, out
):
    nc = tc.nc
    with ExitStack() as ctx:
        sb = ctx.enter_context(tc.tile_pool(name="sb", bufs=1))
        ps = ctx.enter_context(tc.psum_pool(name="ps", bufs=1))
        ctx.enter_context(tc.manual_schedule())

        def sbuf(name, shape, dtype):
            return sb.tile(shape, dtype, name=name, align_bytes=64)

        c_raw0 = sbuf("c_raw0", [P, 2 * N], U8)
        c_raw1 = sbuf("c_raw1", [P, (GROUPS - 1) * 2 * N], U8)
        cs_raw = sbuf("cs_raw", [P, T], U8)
        c_codes = [sbuf("c_codes%d" % g, [P, 2 * N], U8) for g in range(GROUPS)]
        c_plane = [sbuf("c_plane%d" % g, [P, N], U8) for g in range(GROUPS)]
        a_codes0 = sbuf("a_codes0", [P, 2 * N], U8)
        a_codes1 = sbuf("a_codes1", [P, (CHUNKS - 1) * 2 * N], U8)
        a_plane = sbuf("a_plane", [P, PIX], U8)
        d_codes = sbuf("d_codes", [P, GROUPS, K], U32)
        d_plane = sbuf("d_plane", [P, GROUPS, K], U8)
        fw_raw = sbuf("fw_raw", [P, GROUPS, 16], BF16)
        neg_fw = sbuf("neg_fw", [P, GROUPS, PACK], F32)
        step_raw = sbuf("step_raw", [P, M_TILES, 16], BF16)
        step_f32 = sbuf("step_f32", [P, M_TILES], F32)
        warm_in = sbuf("warm_in", [P, 1], F32)
        warm_out = sbuf("warm_out", [P, 1], F32)
        mv = [sbuf("mv%d" % s, [P, PACK, N], BF16) for s in range(STEPS)]
        mw = [sbuf("mw%d" % i, [P, N], F32) for i in range(MW_BUFS)]
        hs = [sbuf("hs%d" % i, [P, PACK, N], BF16) for i in range(HS_BUFS)]
        grouped = [sbuf("grouped%d" % i, [P, N, PACK], BF16) for i in range(2)]
        h_codes = [sbuf("h_codes%d" % s, [P, N], U32) for s in range(STEPS)]
        h_plane = [sbuf("h_plane%d" % s, [P, N], U8) for s in range(STEPS)]
        res = [sbuf("res%d" % i, [P, N], F32) for i in range(OUT_BUFS)]
        e_bank = [ps.tile([P, N], F32, name="e_bank%d" % t) for t in range(PACK)]
        o_bank = [ps.tile([P, N], F32, name="o_bank%d" % m) for m in range(M_TILES)]

        def load_movie(s):
            c, g = divmod(s, GROUPS)
            rows = movie[g * N : (g + 1) * N, c * N : (c + 1) * N]
            nc.sync.dma_start(out=mv[s][:], in_=rows.rearrange("(p t) n -> p t n", t=PACK))

        def load_plane(plane, rows):
            for r in range(4):
                nc.sync.dma_start(out=plane[r:P:32].bitcast(I32), in_=rows[r:16:4].bitcast(I32))

        def order_c_codes(g):
            raw = c_raw0[:] if g == 0 else c_raw1[:, (g - 1) * 2 * N : g * 2 * N]
            nc.vector.tensor_copy(
                out=c_codes[g][:].rearrange("p (t m b) -> p t m b", t=PACK, b=2),
                in_=raw.rearrange("p (m t b) -> p t m b", t=PACK, b=2),
            )

        def order_c_plane(g):
            nc.vector.tensor_copy(
                out=c_plane[g][:].rearrange("p (t m) -> p t m", t=PACK),
                in_=cs_raw[:, g * N : (g + 1) * N].rearrange("p (m t) -> p t m", t=PACK),
            )

        def model(s, t):
            c, g = divmod(s, GROUPS)
            a_chunk = a_codes0[:] if c == 0 else a_codes1[:, (c - 1) * 2 * N : c * 2 * N]
            nc.tensor.matmul_mx(
                out=e_bank[t][:],
                lhsT=c_codes[g][:, t * 2 * P : (t + 1) * 2 * P].bitcast(FP4X4),
                lhsT_scale=c_plane[g][:, t * P : (t + 1) * P],
                rhs=a_chunk.bitcast(FP4X4),
                rhs_scale=a_plane[:, c * N : (c + 1) * N],
                start=True,
                stop=True,
            )

        def weigh_movie(s, t, on_vector):
            g = s % GROUPS
            dst = mw[(s * PACK + t) % MW_BUFS]
            if on_vector:
                nc.vector.tensor_scalar(
                    out=dst[:], in0=mv[s][:, t, :], scalar1=neg_fw[:, g, t : t + 1], scalar2=None, op0=ALU.mult
                )
            else:
                nc.scalar.activation(out=dst[:], in_=mv[s][:, t, :], func=COPY, scale=neg_fw[:, g, t : t + 1])

        scalar_mw = [(s, t) for s in range(STEPS) for t in range(PACK) if (s, t) not in VEC_MW]

        def weigh_on_scalar(first, count):
            for s, t in scalar_mw[first : first + count]:
                weigh_movie(s, t, False)

        def residual(s, t):
            g = s % GROUPS
            nc.vector.scalar_tensor_tensor(
                out=hs[s % HS_BUFS][:, t, :],
                in0=e_bank[t][:],
                scalar=neg_fw[:, g, t : t + 1],
                in1=mw[(s * PACK + t) % MW_BUFS][:],
                op0=ALU.mult,
                op1=ALU.subtract,
            )

        def rows_of(s, lo, hi):
            return hs[s % HS_BUFS][:, :, lo:hi].rearrange("p t n -> p n t")

        def interleave_by_fours(engine_copy, s, lo, hi):
            engine_copy(
                out=grouped[s % 2][:, lo:hi, :].rearrange("p (c i) t -> p c t i", i=4),
                in_=hs[s % HS_BUFS][:, :, lo:hi].rearrange("p t (c i) -> p c t i", i=4),
            )

        def quantize(s, lo, hi):
            nc.vector.quantize_mx(
                out=h_codes[s][:, lo:hi].bitcast(FP8X4),
                scales=h_plane[s][:, lo:hi],
                in_=grouped[s % 2][:, lo:hi, :].rearrange("p n t -> p (n t)"),
            )

        def update(c, g, m):
            s = c * GROUPS + g
            nc.tensor.matmul_mx(
                out=o_bank[m][:],
                lhsT=d_codes[:, g, m * P : (m + 1) * P].bitcast(FP8X4),
                lhsT_scale=d_plane[:, g, m * P : (m + 1) * P],
                rhs=h_codes[s][:].bitcast(FP8X4),
                rhs_scale=h_plane[s][:],
                start=(g == 0),
                stop=(g == GROUPS - 1),
            )

        def finish(c, m, on_vector):
            dst = res[(c * M_TILES + m) % OUT_BUFS]
            if on_vector:
                nc.vector.tensor_scalar(
                    out=dst[:], in0=o_bank[m][:], scalar1=step_f32[:, m : m + 1], scalar2=None, op0=ALU.mult
                )
            else:
                nc.scalar.activation(out=dst[:], in_=o_bank[m][:], func=COPY, scale=step_f32[:, m : m + 1])
            nc.sync.dma_start(out=out[m * P : (m + 1) * P, c * N : (c + 1) * N], in_=dst[:])

        sums_at = {s: [] for s in range(STEPS)}
        for m in range(M_TILES):
            sums_at[5 + m].append((0, m))
            sums_at[9 + m].append((1, m))
            sums_at[13 + m // 2].append((2, m))

        nc.vector.memset(cs_raw[:].bitcast(I32), 0)
        nc.vector.memset(a_plane[:].bitcast(I32), 0)
        nc.vector.memset(d_plane[:].rearrange("p g n -> p (g n)").bitcast(I32), 0)
        nc.gpsimd.memset(warm_in[:], 0.0)
        nc.scalar.activation(out=warm_out[:], in_=warm_in[:], func=COPY, scale=-1.0)

        nc.sync.dma_start(out=c_raw0[:].bitcast(I32), in_=c_words[0][:, 0 : 2 * N].bitcast(I32))
        load_plane(cs_raw, c_scales[0])
        nc.sync.dma_start(out=c_raw1[:].bitcast(I32), in_=c_words[0][:, 2 * N :].bitcast(I32))
        nc.sync.dma_start(out=fw_raw[:, :, 0:PACK], in_=frame_weight.rearrange("(g p t) -> p g t", g=GROUPS, t=PACK))
        load_movie(0)
        nc.sync.dma_start(out=a_codes0[:].bitcast(I32), in_=a_words[0][:, 0 : 2 * N].bitcast(I32))
        load_plane(a_plane, a_scales[0])
        for s in range(1, 6):
            load_movie(s)
        nc.sync.dma_start(out=a_codes1[:].bitcast(I32), in_=a_words[0][:, 2 * N :].bitcast(I32))
        load_movie(6)
        load_plane(d_plane, d_scales.rearrange("g q n -> q g n"))
        with nc.allow_non_contiguous_dma(reason="one step value for each partition"):
            nc.sync.dma_start(out=step_raw[:, :, 0:1], in_=step.rearrange("(m p o) -> p m o", p=P, o=1))
        nc.sync.dma_start(out=d_codes[:].bitcast(I32), in_=d_words.rearrange("g p n t -> p g (n t)").bitcast(I32))
        for s in range(7, STEPS):
            load_movie(s)

        nc.scalar.activation(out=neg_fw[:], in_=fw_raw[:, :, 0:PACK], func=COPY, scale=-1.0)
        order_c_codes(0)
        order_c_plane(0)
        for t in range(PACK):
            model(0, t)
        for g in range(1, GROUPS):
            order_c_codes(g)
        for g in range(1, GROUPS):
            order_c_plane(g)
        weigh_on_scalar(0, SCALAR_MW_HEAD)

        for s in range(STEPS):
            passes = [(c, g, m) for (c, m) in sums_at[s] for g in range(GROUPS)]
            if s == STEPS - 1:
                passes = [(CHUNKS - 1, g, m) for g in range(2) for m in range(M_TILES)]
            share = len(passes) // PACK
            for item in passes[:share]:
                update(*item)
            for t in range(PACK):
                residual(s, t)
                if s == 0 and t in (1, 2):
                    for item in VEC_MW[(t - 1) * 4 : t * 4]:
                        weigh_movie(*item, True)
                for item in passes[(t + 1) * share : (t + 2) * share]:
                    update(*item)
                if s + 1 < STEPS:
                    model(s + 1, t)
            if s > 0:
                quantize(s - 1, 0, N)
            if s < STEPS - 1:
                nc.gpsimd.tensor_scalar(
                    out=grouped[s % 2][:, 0:POOL_PIX, :],
                    in0=rows_of(s, 0, POOL_PIX),
                    scalar1=1.0,
                    scalar2=0.0,
                    op0=ALU.mult,
                    op1=ALU.add,
                )
                interleave_by_fours(nc.scalar.copy, s, POOL_PIX, N)
            else:
                interleave_by_fours(nc.scalar.copy, s, LAST_VEC_PIX, N)
            if s == 3:
                nc.scalar.activation(out=step_f32[:], in_=step_raw[:, :, 0], func=COPY)
            for c, m in sums_at[s]:
                finish(c, m, False)
            weigh_on_scalar(SCALAR_MW_HEAD + sum(SCALAR_MW_AFTER[:s]), SCALAR_MW_AFTER[s])

        last = STEPS - 1
        for m in range(M_TILES):
            update(CHUNKS - 1, GROUPS - 2, m)
        interleave_by_fours(nc.vector.tensor_copy, last, 0, LAST_VEC_PIX)
        quantize(last, LAST_VEC_PIX, N)
        quantize(last, 0, LAST_VEC_PIX)
        for m in range(M_TILES):
            update(CHUNKS - 1, GROUPS - 1, m)
        for m in range(M_TILES):
            finish(CHUNKS - 1, m, m % 2 == 0)
